import numpy as np, ml_dtypes
CORES = [3,11,19,27,35,43]
N = 6
import mx_ref
BF = ml_dtypes.bfloat16
def entries(a):
    return np.ascontiguousarray(a.T).reshape(-1)
def table(e):
    return np.ascontiguousarray(np.reshape(e, (-1, 16)).T).astype(np.int32)
def gentries(a):
    return np.ascontiguousarray(a.reshape(8, 16, -1).transpose(0, 2, 1)).reshape(8, -1)
def gtable(e):
    e = np.asarray(e); return np.ascontiguousarray(e.reshape(8, -1, 16).transpose(0, 2, 1)).reshape(128, -1).astype(np.int32)
def cols(t, e):
    v = np.concatenate([t.reshape(128, -1, 4), np.zeros((128, 1, 4), BF)], axis=1)
    return np.ascontiguousarray(v[:, e]).reshape(128, -1)
def gcols(t, e):
    v = np.concatenate([t.reshape(8, 16, -1, 4), np.zeros((8, 16, 1, 4), BF)], axis=2)
    return np.ascontiguousarray(np.stack([v[g][:, e[g]] for g in range(8)])).reshape(128, -1)
def cut(t, i, w=512):
    return t[:, w * i:w * i + w]
def f(rng, *shape):
    return mx_ref.flush((rng.standard_normal(shape, dtype=np.float32) * np.exp2(rng.integers(-2, 3, shape[:-1] + (1,)))).astype(BF))
def wide(rng, *shape, cols=0):
    v = rng.standard_normal(shape, dtype=np.float32) * np.exp2(rng.integers(-12, 13, shape)).astype(np.float32)
    if cols: v *= np.repeat(np.exp2(rng.integers(-cols, cols + 1, shape[:-2] + (1, shape[-1] // 4))) * (rng.random(shape[:-2] + (1, shape[-1] // 4)) > 0.0625), 4, axis=-1).astype(np.float32)
    return mx_ref.flush(v.astype(BF))
T, CAPP, S, O = 256, 96, 512, 2
def lists(rng, kind=""):
    sn = np.full((N, N, CAPP), -1)
    for s in range(N):
        for d in range(N):
            n = CAPP if kind == "foreign" else 0 if kind == "own" else int(rng.integers(0, CAPP + 1))
            if d != s: sn[s, d, rng.permutation(CAPP)[:n]] = rng.integers(0, T, n)
    if kind == "one":
        s, d = rng.permutation(N)[:2]; sn[s, d] = rng.integers(0, T)
    ql = []
    for r in range(N):
        slots = T + np.flatnonzero(sn[:, r].reshape(-1) >= 0)
        if kind == "foreign": e = rng.permutation(np.resize(slots, 4 * S)).reshape(4, S)
        elif kind == "own": e = rng.integers(0, T, (4, S))
        else: e = rng.choice(np.concatenate([np.arange(T), slots]), (4, S))
        if kind == "whole": e = np.repeat(e[:1], 4, axis=0)
        if kind == "one":
            for u in rng.permutation(4)[:int(rng.integers(1, 5))]: e[u] = e[u, 0]
        ql.append(gtable(np.repeat(e, 2, axis=0)))
    return {"sn": np.stack([table(sn[s].reshape(-1)) for s in range(N)]), "ql": np.stack(ql)}
def setup_inputs(rng):
    return {"x": f(rng, N, 128, 4 * T), "w": f(rng, N, 128, O * 512), **lists(rng)}
def setup_inputs_whole(rng):
    return {**setup_inputs(rng), **lists(rng, "whole")}
def setup_inputs_foreign(rng):
    return {**setup_inputs(rng), **lists(rng, "foreign")}
def setup_inputs_own(rng):
    return {**setup_inputs(rng), **lists(rng, "own")}
def setup_inputs_one(rng):
    return {**setup_inputs(rng), **lists(rng, "one")}
def setup_inputs_spread(rng):
    d = setup_inputs(rng); d["x"] = wide(rng, N, 128, 4 * T, cols=8); return d
def check_inputs(d):
    b = []; to = [entries(d["sn"][s]).reshape(N, CAPP) for s in range(N)]
    for r in range(N):
        if to[r].min() < -1 or to[r].max() >= T or (to[r][r] != -1).any(): b.append("sn")
        e = gentries(d["ql"][r]); there = np.concatenate([np.ones(T, bool)] + [to[s][r] >= 0 for s in range(N)])
        if e.min() < 0 or e.max() >= T + N * CAPP or not there[np.clip(e, 0, T + N * CAPP - 1)].all() or (e[0::2] != e[1::2]).any(): b.append("ql")
    return b
def reference(x, w, sn, ql):
    to = [entries(sn[s]).reshape(N, CAPP) for s in range(N)]
    y = np.zeros((N, 128, O * S), np.float32)
    for r in range(N):
        have = np.concatenate([x[r]] + [cols(x[s], to[s][r]) for s in range(N)], axis=1)
        V = mx_ref.quantize(gcols(have, gentries(ql[r])))
        for o in range(O): y[r][:, S * o:S * o + S] = mx_ref.matmul(mx_ref.quantize(np.ascontiguousarray(cut(w[r], o))), V)
    return {"y": y}

@@ -1,0 +1,190 @@
+from concourse.bass import DstId, RemoteDMATransfer
+from concourse.mybir import dt, ActivationFunctionType
+
+N = 6
+XC, CAPP, S, O = 256, 96, 512, 2
+PIECES = [(0, 256), (256, 512)]
+K = CAPP // 16
+HV = XC + N * CAPP
+
+SCRATCH = {
+    "xt": ("sbuf", [128, 4 * XC], "bfloat16"),
+    "wt": ("sbuf", [128, O * 512], "bfloat16"),
+    "snt": ("sbuf", [128, N * K], "int32"),
+    "qlt": ("sbuf", [128, S // 16], "int32"),
+    "offs": ("sbuf", [128, N * K], "uint16"),
+    "offv": ("sbuf", [128, S // 16], "uint16"),
+    "qx": ("sbuf", [128, XC], "float8_e4m3fn_x4"),
+    "sx": ("sbuf", [128, XC], "uint8"),
+    "qw": ("sbuf", [128, O * 128], "float8_e4m3fn_x4"),
+    "sw": ("sbuf", [128, O * 128], "uint8"),
+    "qs": ("sbuf", [128, N * CAPP], "float8_e4m3fn_x4"),
+    "ss": ("sbuf", [128, N * CAPP], "uint8"),
+    "have": ("sbuf", [128, HV], "float8_e4m3fn_x4"),
+    "haves": ("sbuf", [128, HV], "uint8"),
+    "qv": ("sbuf", [128, S], "float8_e4m3fn_x4"),
+    "sv": ("sbuf", [128, S], "uint8"),
+    "yt": ("sbuf", [128, O * S], "float32"),
+    "acc": ("psum", [128, 512 * O * len(PIECES)], "float32"),
+}
+SEMAPHORES = ["ldx", "ldsn", "ldql", "ldw", "offs", "qx", "have", "qw", "offv", "pc0", "pc1", "ps0", "ps1",
+              "arrc", "arrs", "sent", "sty", "sta"] + \
+             ["vc%d" % i for i in range(len(PIECES))] + ["vs%d" % i for i in range(len(PIECES))] + \
+             ["mm%d_%d" % (o, i) for o in range(O) for i in range(len(PIECES))] + \
+             ["cp%d_%d" % (o, i) for o in range(O) for i in range(len(PIECES))]
+
+
+def bits(engines):
+    m = 0
+    for e in engines:
+        m |= 1 << e
+    return m
+
+
+def roads(src, T, topo):
+    c = T.cores[src]
+    first = [d for d in range(N) if d != src and topo.mates(topo.chip(c), topo.chip(T.cores[d]))][0]
+    rest = [(src + k) % N for k in range(1, N) if (src + k) % N != first]
+    e0 = topo.engines(c, T.cores[first])
+    fused = []
+    for i, d in enumerate(rest):
+        e = topo.engines(c, T.cores[d])
+        w = len(e) // len(rest)
+        fused.append((d, e[w * i:w * i + w]))
+    return (first, e0), fused
+
+
+def runs(ranks):
+    out = []
+    for d in sorted(ranks):
+        if out and out[-1][1] == d:
+            out[-1] = (out[-1][0], d + 1)
+        else:
+            out.append((d, d + 1))
+    return out
+
+
+def rank_program(g, core, T, topo):
+    r = T.rank_of(core)
+    if r is None:
+        return
+    sem = T.sem
+    COPY = ActivationFunctionType.Copy
+    (m, me), fused = roads(r, T, topo)
+    rest = runs([d for d, _ in fused])
+    np_ = len(PIECES)
+
+    g.sync.dma_start(T.xt[:], T.x[:]).then_inc(sem.ldx, 16)
+    for k in range(8):
+        q = g.sync if k >= 5 else g.scalar
+        q.dma_start(T.snt[16 * k:16 * k + 16, :], T.sn[:]).then_inc(sem.ldsn, 16)
+    g.sync.dma_start(T.wt[:], T.w[:]).then_inc(sem.ldw, 16)
+    g.sync.dma_start(T.qlt[:], T.ql[:]).then_inc(sem.ldql, 16)
+
+    def slots(d0, d1):
+        return slice(CAPP * d0, CAPP * d1), slice(K * d0, K * d1)
+
+    v = g.vector
+    v.wait_ge(sem.ldsn, 128)
+    v.tensor_copy(T.offs[:], T.snt[:]).then_inc(sem.offs, 1)
+    v.wait_ge(sem.ldx, 16)
+    v.quantize_mx(T.qx[:], T.sx[:], T.xt[:]).then_inc(sem.qx, 1)
+    v.wait_ge(sem.offs, 1)
+    v.wait_ge(sem.qx, 1)
+    for name, todo in (("pc0", [(m, m + 1)]), ("pc1", rest)):
+        for a, b in todo:
+            c, o = slots(a, b)
+            v.tensor_copy(T.qs[:, c].bitcast(dt.uint32),
+                          T.qx[:].bitcast(dt.uint32).indirect(T.offs[:, o])).then_inc(sem[name], 1)
+    v.quantize_mx(T.have[:, 0:XC], T.haves[:, 0:XC], T.xt[:]).then_inc(sem.have, 1)
+    v.wait_ge(sem.ldw, 16)
+    v.quantize_mx(T.qw[:], T.sw[:], T.wt[:]).then_inc(sem.qw, 1)
+    v.wait_ge(sem.ldql, 16)
+    v.tensor_copy(T.offv[:], T.qlt[:]).then_inc(sem.offv, 1)
+
+    s = g.scalar
+    s.wait_ge(sem.offs, 1)
+    s.wait_ge(sem.qx, 1)
+    for name, todo in (("ps0", [(m, m + 1)]), ("ps1", rest)):
+        for a, b in todo:
+            c, o = slots(a, b)
+            s.activation(T.ss[:, c], T.sx[:].indirect(T.offs[:, o]), COPY).then_inc(sem[name], 1)
+
+    here = slice(XC + CAPP * r, XC + CAPP * r + CAPP)
+
+    def ends(d, scales):
+        c = slice(CAPP * d, CAPP * d + CAPP)
+        if scales:
+            return T.haves[:, here], T.ss[:, c], sem.arrs
+        return T.have[:, here].bitcast(dt.uint8), T.qs[:, c].bitcast(dt.uint8), sem.arrc
+
+    def single(scales):
+        out, src, arr = ends(m, scales)
+        rid, pid, _ = topo.addr(T.cores[m])
+        g.remote_dma(out, src, arr, sem.sent, pid, rid, bits(me))
+
+    def four(scales):
+        ts = []
+        for d, e in fused:
+            out, src, arr = ends(d, scales)
+            rid, pid, _ = topo.addr(T.cores[d])
+            ts.append(RemoteDMATransfer(dst_ids=[DstId(rid=rid, pnc=pid)], dma_engine_mask=bits(e),
+                                        remote_sem=arr, srcs=[src], dsts=[out]))
+        g.remote_dma_fused(ts, local_sem=sem.sent)
+
+    g.wait_ge(sem.pc0, 1)
+    single(False)
+    g.wait_ge(sem.pc1, len(rest))
+    four(False)
+    g.wait_ge(sem.ps1, len(rest))
+    four(True)
+    g.wait_ge(sem.ps0, 1)
+    single(True)
+    total = 2 * (len(me) + sum(len(e) for _, e in fused))
+    g.wait_ge(sem.sent, total)
+
+    come = 0
+    for q in range(N):
+        if q != r:
+            (f, fe), fs = roads(q, T, topo)
+            come += sum(len(e) for d, e in [(f, fe)] + fs if d == r)
+
+    v.wait_ge(sem.offv, 1)
+    v.wait_ge(sem.have, 1)
+    v.wait_ge(sem.arrc, come)
+    for i, (a, b) in enumerate(PIECES):
+        v.tensor_copy(T.qv[:, a:b].bitcast(dt.uint32),
+                      T.have[:].bitcast(dt.uint32).indirect(T.offv[:, a // 16:b // 16])).then_inc(sem["vc%d" % i], 1)
+    s.wait_ge(sem.offv, 1)
+    s.wait_ge(sem.have, 1)
+    s.wait_ge(sem.arrs, come)
+    for i, (a, b) in enumerate(PIECES):
+        s.activation(T.sv[:, a:b], T.haves[:].indirect(T.offv[:, a // 16:b // 16]), COPY).then_inc(sem["vs%d" % i], 1)
+
+    t = g.tensor
+    t.wait_ge(sem.qw, 1)
+    for i, (a, b) in enumerate(PIECES):
+        t.wait_ge(sem["vc%d" % i], 1)
+        t.wait_ge(sem["vs%d" % i], 1)
+        for o in range(O):
+            bank = 512 * (O * i + o)
+            t.matmul_mx(T.acc[:, bank:bank + b - a], T.qw[:, 128 * o:128 * o + 128], T.sw[:, 128 * o:128 * o + 128],
+                        T.qv[:, a:b], T.sv[:, a:b], True, True).then_inc(sem["mm%d_%d" % (o, i)], 1)
+
+    for i, (a, b) in enumerate(PIECES):
+        for o in range(O):
+            bank = 512 * (O * i + o)
+            src, dst = T.acc[:, bank:bank + b - a], slice(S * o + a, S * o + b)
+            mm, cp = sem["mm%d_%d" % (o, i)], sem["cp%d_%d" % (o, i)]
+            if o == 0:
+                v.wait_ge(mm, 1)
+                v.tensor_copy(T.yt[:, dst], src).then_inc(cp, 1)
+                g.sync.wait_ge(cp, 1)
+                g.sync.dma_start(T.y[:, dst], T.yt[:, dst]).then_inc(sem.sty, 16)
+            else:
+                s.wait_ge(mm, 1)
+                s.activation(T.yt[:, dst], src, COPY).then_inc(cp, 1)
+                s.wait_ge(cp, 1)
+                s.dma_start(T.y[:, dst], T.yt[:, dst]).then_inc(sem.sta, 16)
+    g.sync.wait_ge(sem.sty, 16 * np_)
+    s.wait_ge(sem.sta, 16 * np_)

@@ -3,7 +3,7 @@ from concourse.mybir import dt, ActivationFunctionType
 
 N = 6
 XC, CAPP, S, O = 256, 96, 512, 2
-PIECES = [(0, 256), (256, 512)]
+PIECES = [(128, "vv"), (192, "vs"), (192, "vs")]
 K = CAPP // 16
 HV = XC + N * CAPP
 
@@ -28,10 +28,9 @@ SCRATCH = {
     "acc": ("psum", [128, 512 * O * len(PIECES)], "float32"),
 }
 SEMAPHORES = ["ldx", "ldsn", "ldql", "ldw", "offs", "qx", "have", "qw", "offv", "pc0", "pc1", "ps0", "ps1",
-              "arrc", "arrs", "sent", "sty", "sta"] + \
+              "arrc", "arrs", "sent", "sty"] + \
              ["vc%d" % i for i in range(len(PIECES))] + ["vs%d" % i for i in range(len(PIECES))] + \
-             ["mm%d_%d" % (o, i) for o in range(O) for i in range(len(PIECES))] + \
-             ["cp%d_%d" % (o, i) for o in range(O) for i in range(len(PIECES))]
+             ["mm%d" % i for i in range(O * len(PIECES))] + ["cp%d" % i for i in range(O * len(PIECES))]
 
 
 def bits(engines):
@@ -43,7 +42,7 @@ def bits(engines):
 
 def roads(src, T, topo):
     c = T.cores[src]
-    first = [d for d in range(N) if d != src and topo.mates(topo.chip(c), topo.chip(T.cores[d]))][0]
+    first = (src + N // 2) % N
     rest = [(src + k) % N for k in range(1, N) if (src + k) % N != first]
     e0 = topo.engines(c, T.cores[first])
     fused = []
@@ -72,11 +71,10 @@ def rank_program(g, core, T, topo):
     COPY = ActivationFunctionType.Copy
     (m, me), fused = roads(r, T, topo)
     rest = runs([d for d, _ in fused])
-    np_ = len(PIECES)
 
     g.sync.dma_start(T.xt[:], T.x[:]).then_inc(sem.ldx, 16)
     for k in range(8):
-        q = g.sync if k >= 5 else g.scalar
+        q = g.sync if k % 2 else g.scalar
         q.dma_start(T.snt[16 * k:16 * k + 16, :], T.sn[:]).then_inc(sem.ldsn, 16)
     g.sync.dma_start(T.wt[:], T.w[:]).then_inc(sem.ldw, 16)
     g.sync.dma_start(T.qlt[:], T.ql[:]).then_inc(sem.ldql, 16)
@@ -85,12 +83,12 @@ def rank_program(g, core, T, topo):
         return slice(CAPP * d0, CAPP * d1), slice(K * d0, K * d1)
 
     v = g.vector
-    v.wait_ge(sem.ldsn, 128)
-    v.tensor_copy(T.offs[:], T.snt[:]).then_inc(sem.offs, 1)
     v.wait_ge(sem.ldx, 16)
     v.quantize_mx(T.qx[:], T.sx[:], T.xt[:]).then_inc(sem.qx, 1)
-    v.wait_ge(sem.offs, 1)
+    v.wait_ge(sem.ldsn, 128)
+    v.tensor_copy(T.offs[:], T.snt[:]).then_inc(sem.offs, 1)
     v.wait_ge(sem.qx, 1)
+    v.wait_ge(sem.offs, 1)
     for name, todo in (("pc0", [(m, m + 1)]), ("pc1", rest)):
         for a, b in todo:
             c, o = slots(a, b)
@@ -103,8 +101,8 @@ def rank_program(g, core, T, topo):
     v.tensor_copy(T.offv[:], T.qlt[:]).then_inc(sem.offv, 1)
 
     s = g.scalar
-    s.wait_ge(sem.offs, 1)
     s.wait_ge(sem.qx, 1)
+    s.wait_ge(sem.offs, 1)
     for name, todo in (("ps0", [(m, m + 1)]), ("ps1", rest)):
         for a, b in todo:
             c, o = slots(a, b)
@@ -140,8 +138,7 @@ def rank_program(g, core, T, topo):
     four(True)
     g.wait_ge(sem.ps0, 1)
     single(True)
-    total = 2 * (len(me) + sum(len(e) for _, e in fused))
-    g.wait_ge(sem.sent, total)
+    g.wait_ge(sem.sent, 2 * (len(me) + sum(len(e) for _, e in fused)))
 
     come = 0
     for q in range(N):
@@ -149,42 +146,39 @@ def rank_program(g, core, T, topo):
             (f, fe), fs = roads(q, T, topo)
             come += sum(len(e) for d, e in [(f, fe)] + fs if d == r)
 
+    ends_at = [sum(p[0] for p in PIECES[:i + 1]) for i in range(len(PIECES))]
+    cols = [(e - p[0], e) for e, p in zip(ends_at, PIECES)]
     v.wait_ge(sem.offv, 1)
     v.wait_ge(sem.have, 1)
     v.wait_ge(sem.arrc, come)
-    for i, (a, b) in enumerate(PIECES):
+    for i, (a, b) in enumerate(cols):
         v.tensor_copy(T.qv[:, a:b].bitcast(dt.uint32),
                       T.have[:].bitcast(dt.uint32).indirect(T.offv[:, a // 16:b // 16])).then_inc(sem["vc%d" % i], 1)
     s.wait_ge(sem.offv, 1)
     s.wait_ge(sem.have, 1)
     s.wait_ge(sem.arrs, come)
-    for i, (a, b) in enumerate(PIECES):
-        s.activation(T.sv[:, a:b], T.haves[:].indirect(T.offv[:, a // 16:b // 16]), COPY).then_inc(sem["vs%d" % i], 1)
-
     t = g.tensor
     t.wait_ge(sem.qw, 1)
-    for i, (a, b) in enumerate(PIECES):
+    for i, (a, b) in enumerate(cols):
+        s.activation(T.sv[:, a:b], T.haves[:].indirect(T.offv[:, a // 16:b // 16]), COPY).then_inc(sem["vs%d" % i], 1)
         t.wait_ge(sem["vc%d" % i], 1)
         t.wait_ge(sem["vs%d" % i], 1)
         for o in range(O):
-            bank = 512 * (O * i + o)
-            t.matmul_mx(T.acc[:, bank:bank + b - a], T.qw[:, 128 * o:128 * o + 128], T.sw[:, 128 * o:128 * o + 128],
-                        T.qv[:, a:b], T.sv[:, a:b], True, True).then_inc(sem["mm%d_%d" % (o, i)], 1)
+            k = O * i + o
+            t.matmul_mx(T.acc[:, 512 * k:512 * k + b - a], T.qw[:, 128 * o:128 * o + 128],
+                        T.sw[:, 128 * o:128 * o + 128], T.qv[:, a:b], T.sv[:, a:b],
+                        True, True).then_inc(sem["mm%d" % k], 1)
 
-    for i, (a, b) in enumerate(PIECES):
+    for i, (a, b) in enumerate(cols):
         for o in range(O):
-            bank = 512 * (O * i + o)
-            src, dst = T.acc[:, bank:bank + b - a], slice(S * o + a, S * o + b)
-            mm, cp = sem["mm%d_%d" % (o, i)], sem["cp%d_%d" % (o, i)]
-            if o == 0:
-                v.wait_ge(mm, 1)
-                v.tensor_copy(T.yt[:, dst], src).then_inc(cp, 1)
-                g.sync.wait_ge(cp, 1)
-                g.sync.dma_start(T.y[:, dst], T.yt[:, dst]).then_inc(sem.sty, 16)
+            k = O * i + o
+            src, dst = T.acc[:, 512 * k:512 * k + b - a], slice(S * o + a, S * o + b)
+            if PIECES[i][1][o] == "v":
+                v.wait_ge(sem["mm%d" % k], 1)
+                v.tensor_copy(T.yt[:, dst], src).then_inc(sem["cp%d" % k], 1)
             else:
-                s.wait_ge(mm, 1)
-                s.activation(T.yt[:, dst], src, COPY).then_inc(cp, 1)
-                s.wait_ge(cp, 1)
-                s.dma_start(T.y[:, dst], T.yt[:, dst]).then_inc(sem.sta, 16)
-    g.sync.wait_ge(sem.sty, 16 * np_)
-    s.wait_ge(sem.sta, 16 * np_)
+                s.wait_ge(sem["mm%d" % k], 1)
+                s.activation(T.yt[:, dst], src, COPY).then_inc(sem["cp%d" % k], 1)
+            g.sync.wait_ge(sem["cp%d" % k], 1)
+            g.sync.dma_start(T.y[:, dst], T.yt[:, dst]).then_inc(sem.sty, 16)
+    g.sync.wait_ge(sem.sty, 16 * O * len(PIECES))

from concourse.bass import DstId, RemoteDMATransfer
from concourse.mybir import dt, ActivationFunctionType

N = 6
XC, CAPP, S, O = 256, 96, 512, 2
PIECES = [(128, "vv"), (192, "vs"), (192, "vs")]
K = CAPP // 16
HV = XC + N * CAPP

SCRATCH = {
    "xt": ("sbuf", [128, 4 * XC], "bfloat16"),
    "wt": ("sbuf", [128, O * 512], "bfloat16"),
    "snt": ("sbuf", [128, N * K], "int32"),
    "qlt": ("sbuf", [128, S // 16], "int32"),
    "offs": ("sbuf", [128, N * K], "uint16"),
    "offv": ("sbuf", [128, S // 16], "uint16"),
    "qx": ("sbuf", [128, XC], "float8_e4m3fn_x4"),
    "sx": ("sbuf", [128, XC], "uint8"),
    "qw": ("sbuf", [128, O * 128], "float8_e4m3fn_x4"),
    "sw": ("sbuf", [128, O * 128], "uint8"),
    "qs": ("sbuf", [128, N * CAPP], "float8_e4m3fn_x4"),
    "ss": ("sbuf", [128, N * CAPP], "uint8"),
    "have": ("sbuf", [128, HV], "float8_e4m3fn_x4"),
    "haves": ("sbuf", [128, HV], "uint8"),
    "qv": ("sbuf", [128, S], "float8_e4m3fn_x4"),
    "sv": ("sbuf", [128, S], "uint8"),
    "yt": ("sbuf", [128, O * S], "float32"),
    "acc": ("psum", [128, 512 * O * len(PIECES)], "float32"),
}
SEMAPHORES = ["ldx", "ldsn", "ldql", "ldw", "offs", "qx", "have", "qw", "offv", "pc0", "pc1", "ps0", "ps1",
              "arrc", "arrs", "sent", "sty"] + \
             ["vc%d" % i for i in range(len(PIECES))] + ["vs%d" % i for i in range(len(PIECES))] + \
             ["mm%d" % i for i in range(O * len(PIECES))] + ["cp%d" % i for i in range(O * len(PIECES))]


def bits(engines):
    m = 0
    for e in engines:
        m |= 1 << e
    return m


def roads(src, T, topo):
    c = T.cores[src]
    first = (src + N // 2) % N
    rest = [(src + k) % N for k in range(1, N) if (src + k) % N != first]
    e0 = topo.engines(c, T.cores[first])
    fused = []
    for i, d in enumerate(rest):
        e = topo.engines(c, T.cores[d])
        w = len(e) // len(rest)
        fused.append((d, e[w * i:w * i + w]))
    return (first, e0), fused


def runs(ranks):
    out = []
    for d in sorted(ranks):
        if out and out[-1][1] == d:
            out[-1] = (out[-1][0], d + 1)
        else:
            out.append((d, d + 1))
    return out


def rank_program(g, core, T, topo):
    r = T.rank_of(core)
    if r is None:
        return
    sem = T.sem
    COPY = ActivationFunctionType.Copy
    (m, me), fused = roads(r, T, topo)
    rest = runs([d for d, _ in fused])

    g.sync.dma_start(T.xt[:], T.x[:]).then_inc(sem.ldx, 16)
    for k in range(8):
        q = g.sync if k % 2 else g.scalar
        q.dma_start(T.snt[16 * k:16 * k + 16, :], T.sn[:]).then_inc(sem.ldsn, 16)
    g.sync.dma_start(T.wt[:], T.w[:]).then_inc(sem.ldw, 16)
    g.sync.dma_start(T.qlt[:], T.ql[:]).then_inc(sem.ldql, 16)

    def slots(d0, d1):
        return slice(CAPP * d0, CAPP * d1), slice(K * d0, K * d1)

    v = g.vector
    v.wait_ge(sem.ldx, 16)
    v.quantize_mx(T.qx[:], T.sx[:], T.xt[:]).then_inc(sem.qx, 1)
    v.wait_ge(sem.ldsn, 128)
    v.tensor_copy(T.offs[:], T.snt[:]).then_inc(sem.offs, 1)
    v.wait_ge(sem.qx, 1)
    v.wait_ge(sem.offs, 1)
    for name, todo in (("pc0", [(m, m + 1)]), ("pc1", rest)):
        for a, b in todo:
            c, o = slots(a, b)
            v.tensor_copy(T.qs[:, c].bitcast(dt.uint32),
                          T.qx[:].bitcast(dt.uint32).indirect(T.offs[:, o])).then_inc(sem[name], 1)
    v.quantize_mx(T.have[:, 0:XC], T.haves[:, 0:XC], T.xt[:]).then_inc(sem.have, 1)
    v.wait_ge(sem.ldw, 16)
    v.quantize_mx(T.qw[:], T.sw[:], T.wt[:]).then_inc(sem.qw, 1)
    v.wait_ge(sem.ldql, 16)
    v.tensor_copy(T.offv[:], T.qlt[:]).then_inc(sem.offv, 1)

    s = g.scalar
    s.wait_ge(sem.qx, 1)
    s.wait_ge(sem.offs, 1)
    for name, todo in (("ps0", [(m, m + 1)]), ("ps1", rest)):
        for a, b in todo:
            c, o = slots(a, b)
            s.activation(T.ss[:, c], T.sx[:].indirect(T.offs[:, o]), COPY).then_inc(sem[name], 1)

    here = slice(XC + CAPP * r, XC + CAPP * r + CAPP)

    def ends(d, scales):
        c = slice(CAPP * d, CAPP * d + CAPP)
        if scales:
            return T.haves[:, here], T.ss[:, c], sem.arrs
        return T.have[:, here].bitcast(dt.uint8), T.qs[:, c].bitcast(dt.uint8), sem.arrc

    def single(scales):
        out, src, arr = ends(m, scales)
        rid, pid, _ = topo.addr(T.cores[m])
        g.remote_dma(out, src, arr, sem.sent, pid, rid, bits(me))

    def four(scales):
        ts = []
        for d, e in fused:
            out, src, arr = ends(d, scales)
            rid, pid, _ = topo.addr(T.cores[d])
            ts.append(RemoteDMATransfer(dst_ids=[DstId(rid=rid, pnc=pid)], dma_engine_mask=bits(e),
                                        remote_sem=arr, srcs=[src], dsts=[out]))
        g.remote_dma_fused(ts, local_sem=sem.sent)

    g.wait_ge(sem.pc0, 1)
    single(False)
    g.wait_ge(sem.pc1, len(rest))
    four(False)
    g.wait_ge(sem.ps1, len(rest))
    four(True)
    g.wait_ge(sem.ps0, 1)
    single(True)
    g.wait_ge(sem.sent, 2 * (len(me) + sum(len(e) for _, e in fused)))

    come = 0
    for q in range(N):
        if q != r:
            (f, fe), fs = roads(q, T, topo)
            come += sum(len(e) for d, e in [(f, fe)] + fs if d == r)

    ends_at = [sum(p[0] for p in PIECES[:i + 1]) for i in range(len(PIECES))]
    cols = [(e - p[0], e) for e, p in zip(ends_at, PIECES)]
    v.wait_ge(sem.offv, 1)
    v.wait_ge(sem.have, 1)
    v.wait_ge(sem.arrc, come)
    for i, (a, b) in enumerate(cols):
        v.tensor_copy(T.qv[:, a:b].bitcast(dt.uint32),
                      T.have[:].bitcast(dt.uint32).indirect(T.offv[:, a // 16:b // 16])).then_inc(sem["vc%d" % i], 1)
    s.wait_ge(sem.offv, 1)
    s.wait_ge(sem.have, 1)
    s.wait_ge(sem.arrs, come)
    t = g.tensor
    t.wait_ge(sem.qw, 1)
    for i, (a, b) in enumerate(cols):
        s.activation(T.sv[:, a:b], T.haves[:].indirect(T.offv[:, a // 16:b // 16]), COPY).then_inc(sem["vs%d" % i], 1)
        t.wait_ge(sem["vc%d" % i], 1)
        t.wait_ge(sem["vs%d" % i], 1)
        for o in range(O):
            k = O * i + o
            t.matmul_mx(T.acc[:, 512 * k:512 * k + b - a], T.qw[:, 128 * o:128 * o + 128],
                        T.sw[:, 128 * o:128 * o + 128], T.qv[:, a:b], T.sv[:, a:b],
                        True, True).then_inc(sem["mm%d" % k], 1)

    for i, (a, b) in enumerate(cols):
        for o in range(O):
            k = O * i + o
            src, dst = T.acc[:, 512 * k:512 * k + b - a], slice(S * o + a, S * o + b)
            if PIECES[i][1][o] == "v":
                v.wait_ge(sem["mm%d" % k], 1)
                v.tensor_copy(T.yt[:, dst], src).then_inc(sem["cp%d" % k], 1)
            else:
                s.wait_ge(sem["mm%d" % k], 1)
                s.activation(T.yt[:, dst], src, COPY).then_inc(sem["cp%d" % k], 1)
            g.sync.wait_ge(sem["cp%d" % k], 1)
            g.sync.dma_start(T.y[:, dst], T.yt[:, dst]).then_inc(sem.sty, 16)
    g.sync.wait_ge(sem.sty, 16 * O * len(PIECES))
